import numpy as np
import ml_dtypes

BF16 = ml_dtypes.bfloat16


def bf(x):
    return np.asarray(x, np.float32).astype(BF16)


def f32(x):
    return np.asarray(x, np.float32)


def f64(x):
    return np.asarray(x).astype(np.float64)


def striped(idx):
    return np.concatenate([l.reshape(-1, 16).T for l in idx])


def rows(idx, k):
    return np.tile(np.repeat(idx, 16, axis=0), (k // (16 * 8), 1))


def look(tab, idx):
    return np.take_along_axis(f64(tab), rows(idx, len(tab)), axis=1)


K, S, V, N = 128, 2048, 1536, 1536


def silu(v):
    return v / (1.0 + np.exp(-v))


def setup_inputs():
    return {"tab": f32(np.random.standard_normal((2, K, S))), "y": f32(np.random.standard_normal((K, V))), "offs": striped(np.stack([np.random.permutation(S)[:N] for _ in range(8)]))}


def reference(tab, y, offs):
    idx = np.stack([g.T.reshape(-1) for g in np.split(offs, 8)])
    x = (look(tab[0], idx) + f64(y)) * (silu(look(tab[1], idx)))
    return x

@@ -1,0 +1,44 @@
+import concourse.mybir as mybir
+
+F32, U16 = mybir.dt.float32, mybir.dt.uint16
+ADD, MULT = mybir.AluOpType.add, mybir.AluOpType.mult
+SILU = mybir.ActivationFunctionType.Silu
+
+P = 128
+PLACES = 2048
+ENTRIES = 1536
+PIECE = 512
+LIST_COLUMNS = 16
+
+FLOPS = 6 * P * ENTRIES
+
+
+def tile_lookup_vg_addsilu_out_kernel(tc, tab, y, offs, out):
+    nc = tc.nc
+    with (
+        tc.tile_pool(name="held", bufs=1) as held,
+        tc.tile_pool(name="ring", bufs=ENTRIES // PIECE) as ring,
+    ):
+        lists = held.tile([P, ENTRIES // LIST_COLUMNS], U16)
+        values = held.tile([P, PLACES], F32)
+        gates = held.tile([P, PLACES], F32)
+        stream = held.tile([P, ENTRIES], F32)
+
+        nc.sync.dma_start(lists[:], offs)
+        nc.sync.dma_start(values[:], tab[0])
+        nc.sync.dma_start(stream[:], y)
+        nc.sync.dma_start(gates[:], tab[1])
+
+        for start in range(0, ENTRIES, PIECE):
+            piece = slice(start, start + PIECE)
+            picks = lists[:, start // LIST_COLUMNS : (start + PIECE) // LIST_COLUMNS]
+
+            summed = ring.tile([P, PIECE], F32)
+            nc.vector.tensor_tensor(summed[:], values[:].indirect(picks), stream[:, piece], ADD)
+
+            gated = ring.tile([P, PIECE], F32)
+            nc.scalar.activation(gated[:], gates[:].indirect(picks), SILU)
+
+            product = ring.tile([P, PIECE], F32)
+            nc.vector.tensor_tensor(product[:], summed[:], gated[:], MULT)
+            nc.sync.dma_start(out[:, piece], product[:])

@@ -24,6 +24,11 @@ def tile_lookup_vg_addsilu_out_kernel(tc, tab, y, offs, out):
         gates = held.tile([P, PLACES], F32)
         stream = held.tile([P, ENTRIES], F32)
 
+        zero = held.tile([P, 1], F32)
+        nc.vector.memset(zero[:], 0.0)
+        warm = held.tile([P, 1], F32)
+        nc.scalar.activation(warm[:], zero[:], SILU)
+
         nc.sync.dma_start(lists[:], offs)
         nc.sync.dma_start(values[:], tab[0])
         nc.sync.dma_start(stream[:], y)

@@ -22,24 +22,27 @@ def tile_lookup_vg_addsilu_out_kernel(tc, tab, y, offs, out):
         lists = held.tile([P, ENTRIES // LIST_COLUMNS], U16)
         values = held.tile([P, PLACES], F32)
         gates = held.tile([P, PLACES], F32)
-        stream = held.tile([P, ENTRIES], F32)
 
         zero = held.tile([P, 1], F32)
         nc.vector.memset(zero[:], 0.0)
         warm = held.tile([P, 1], F32)
         nc.scalar.activation(warm[:], zero[:], SILU)
 
+        pieces = [slice(start, start + PIECE) for start in range(0, ENTRIES, PIECE)]
+        stream = [held.tile([P, PIECE], F32, name=f"stream{i}") for i in range(len(pieces))]
+
         nc.sync.dma_start(lists[:], offs)
         nc.sync.dma_start(values[:], tab[0])
-        nc.sync.dma_start(stream[:], y)
+        nc.sync.dma_start(stream[0][:], y[:, pieces[0]])
         nc.sync.dma_start(gates[:], tab[1])
+        for part, piece in zip(stream[1:], pieces[1:]):
+            nc.sync.dma_start(part[:], y[:, piece])
 
-        for start in range(0, ENTRIES, PIECE):
-            piece = slice(start, start + PIECE)
-            picks = lists[:, start // LIST_COLUMNS : (start + PIECE) // LIST_COLUMNS]
+        for part, piece in zip(stream, pieces):
+            picks = lists[:, piece.start // LIST_COLUMNS : piece.stop // LIST_COLUMNS]
 
             summed = ring.tile([P, PIECE], F32)
-            nc.vector.tensor_tensor(summed[:], values[:].indirect(picks), stream[:, piece], ADD)
+            nc.vector.tensor_tensor(summed[:], values[:].indirect(picks), part[:], ADD)
 
             gated = ring.tile([P, PIECE], F32)
             nc.scalar.activation(gated[:], gates[:].indirect(picks), SILU)

@@ -29,20 +29,21 @@ def tile_lookup_vg_addsilu_out_kernel(tc, tab, y, offs, out):
         nc.scalar.activation(warm[:], zero[:], SILU)
 
         pieces = [slice(start, start + PIECE) for start in range(0, ENTRIES, PIECE)]
-        stream = [held.tile([P, PIECE], F32, name=f"stream{i}") for i in range(len(pieces))]
+        early = held.tile([P, ENTRIES - PIECE], F32)
+        late = held.tile([P, PIECE], F32)
 
         nc.sync.dma_start(lists[:], offs)
         nc.sync.dma_start(values[:], tab[0])
-        nc.sync.dma_start(stream[0][:], y[:, pieces[0]])
+        nc.sync.dma_start(early[:], y[:, : ENTRIES - PIECE])
         nc.sync.dma_start(gates[:], tab[1])
-        for part, piece in zip(stream[1:], pieces[1:]):
-            nc.sync.dma_start(part[:], y[:, piece])
+        nc.sync.dma_start(late[:], y[:, ENTRIES - PIECE :])
 
-        for part, piece in zip(stream, pieces):
+        for piece in pieces:
             picks = lists[:, piece.start // LIST_COLUMNS : piece.stop // LIST_COLUMNS]
+            stream = late[:] if piece is pieces[-1] else early[:, piece]
 
             summed = ring.tile([P, PIECE], F32)
-            nc.vector.tensor_tensor(summed[:], values[:].indirect(picks), part[:], ADD)
+            nc.vector.tensor_tensor(summed[:], values[:].indirect(picks), stream, ADD)
 
             gated = ring.tile([P, PIECE], F32)
             nc.scalar.activation(gated[:], gates[:].indirect(picks), SILU)

import concourse.mybir as mybir

F32, U16 = mybir.dt.float32, mybir.dt.uint16
ADD, MULT = mybir.AluOpType.add, mybir.AluOpType.mult
SILU = mybir.ActivationFunctionType.Silu

P = 128
PLACES = 2048
ENTRIES = 1536
PIECE = 512
LIST_COLUMNS = 16

FLOPS = 6 * P * ENTRIES


def tile_lookup_vg_addsilu_out_kernel(tc, tab, y, offs, out):
    nc = tc.nc
    with (
        tc.tile_pool(name="held", bufs=1) as held,
        tc.tile_pool(name="ring", bufs=ENTRIES // PIECE) as ring,
    ):
        lists = held.tile([P, ENTRIES // LIST_COLUMNS], U16)
        values = held.tile([P, PLACES], F32)
        gates = held.tile([P, PLACES], F32)

        zero = held.tile([P, 1], F32)
        nc.vector.memset(zero[:], 0.0)
        warm = held.tile([P, 1], F32)
        nc.scalar.activation(warm[:], zero[:], SILU)

        pieces = [slice(start, start + PIECE) for start in range(0, ENTRIES, PIECE)]
        early = held.tile([P, ENTRIES - PIECE], F32)
        late = held.tile([P, PIECE], F32)

        nc.sync.dma_start(lists[:], offs)
        nc.sync.dma_start(values[:], tab[0])
        nc.sync.dma_start(early[:], y[:, : ENTRIES - PIECE])
        nc.sync.dma_start(gates[:], tab[1])
        nc.sync.dma_start(late[:], y[:, ENTRIES - PIECE :])

        for piece in pieces:
            picks = lists[:, piece.start // LIST_COLUMNS : piece.stop // LIST_COLUMNS]
            stream = late[:] if piece is pieces[-1] else early[:, piece]

            summed = ring.tile([P, PIECE], F32)
            nc.vector.tensor_tensor(summed[:], values[:].indirect(picks), stream, ADD)

            gated = ring.tile([P, PIECE], F32)
            nc.scalar.activation(gated[:], gates[:].indirect(picks), SILU)

            product = ring.tile([P, PIECE], F32)
            nc.vector.tensor_tensor(product[:], summed[:], gated[:], MULT)
            nc.sync.dma_start(out[:, piece], product[:])
